import numpy as np
import ml_dtypes


def mxq(x, axis, fmt="e4m3"):
    dtype, down = {"e4m3": (ml_dtypes.float8_e4m3fn, 7), "e5m2": (ml_dtypes.float8_e5m2, 14)}[fmt]
    v = np.moveaxis(np.asarray(x, np.float32).astype(ml_dtypes.bfloat16).astype(np.float64), axis, -1)
    blocks = v.reshape(v.shape[:-1] + (-1, 32))
    amax = np.abs(blocks).max(-1, keepdims=True)
    byte = np.maximum(np.where(amax > 0, np.frexp(amax)[1] - 1 + 127, 0) - down, 1)
    scale = np.exp2(byte - 127.0)
    codes = (blocks / scale).astype(np.float32).astype(dtype).astype(np.float64)
    return np.moveaxis((codes * scale).reshape(v.shape), -1, axis)


WIDE = False


def mx_kscale(k):
    if not WIDE:
        return np.ones(k)
    levels = np.array([10, -10, 5, -5, 0])
    if k % 512:
        return np.exp2(np.random.permutation(np.resize(levels, k // 32))).repeat(32)
    a = np.empty((k // 512, 16))
    for p in range(k // 512):
        a[p, :8] = np.random.permutation(np.resize(levels, 8))
        for g in range(8):
            far = levels[np.abs(levels - a[p, g]) >= 10]
            a[p, g + 8] = far[np.random.randint(len(far))]
    return np.exp2(a.ravel()).repeat(32)


def f64(x):
    return np.asarray(x).astype(np.float64)


def striped(idx):
    return np.tile(np.asarray(idx).reshape(-1, 16).T, (8, 1)).astype(np.uint16)


def unstriped(offs):
    return offs[:16].T.reshape(-1).astype(np.int64)


E2M1 = np.array([0.0, 0.5, 1.0, 1.5, 2.0, 3.0, 4.0, 6.0, -0.0, -0.5, -1.0, -1.5, -2.0, -3.0, -4.0, -6.0])


def pack_weight(w, fmt):
    k, n = w.shape
    w = f64(np.asarray(w, np.float32).astype(ml_dtypes.bfloat16)).reshape(k // 32, 32, n)
    amax = np.abs(w).max(1)
    if fmt == "e4m3":
        byte = np.frexp(amax)[1] - 1 + 127 - 7
    else:
        mant, ex = np.frexp(amax / 6.0)
        byte = np.where(mant > 0.5, ex, ex - 1) + 127
    byte = np.clip(np.where(amax > 0, byte, 1), 1, 254)
    scaled = (w * np.exp2(127.0 - byte)[:, None, :]).reshape(k, n).astype(np.float32)
    by_word = np.ascontiguousarray(scaled.reshape(k // 512, 128, 4, n).transpose(0, 1, 3, 2))
    if fmt == "e4m3":
        words = by_word.astype(ml_dtypes.float8_e4m3fn).view(np.uint8)
    else:
        c = by_word.astype(ml_dtypes.float4_e2m1fn).view(np.uint8) & 0xF
        words = (c[..., 0::2] | (c[..., 1::2] << 4)).reshape(k // 512, 128, 2 * n)
    return np.ascontiguousarray(words), np.ascontiguousarray(byte.astype(np.uint8).reshape(k // 512, 16, n))


def unpack_weight(words, scales, fmt):
    g, _, n = scales.shape
    words = np.ascontiguousarray(words).reshape(g, 128, n, -1)
    if fmt == "e4m3":
        vals = words.view(ml_dtypes.float8_e4m3fn).astype(np.float64)
    else:
        nib = np.empty((g, 128, n, 4), np.uint8)
        nib[..., 0::2] = words & 0xF
        nib[..., 1::2] = words >> 4
        vals = E2M1[nib]
    vals = vals * np.repeat(np.exp2(scales.astype(np.float64) - 127.0), 8, axis=1)[..., None]
    return vals.transpose(0, 1, 3, 2).reshape(g * 512, n)


def sigmoid(v):
    return 1.0 / (1.0 + np.exp(-v))


D, T, I, Q, E, U, M = 512, 2048, 512, 512, 512, 1024, 1024


def setup_inputs():
    n = np.random.standard_normal
    idx = np.random.permutation(T)[:I]
    idx2 = np.random.permutation(U)[:I]
    idx3 = np.random.permutation(M)[:I]
    fd = mx_kscale(D)
    fq = mx_kscale(Q)
    keysp = pack_weight(n((D, T)) / fd[:, None], "e4m3")
    return {
        "query": (n((D, Q)) * 0.9 / np.sqrt(D) * fd[:, None]).astype(np.float32),
        "keys_words": keysp[0],
        "keys_scales": keysp[1],
        "query2": (n((D, Q)) * 0.9 / np.sqrt(D) * fd[:, None]).astype(np.float32),
        "notes": (n((D, U)) / fd[:, None]).astype(np.float32),
        "lam": (np.random.uniform(0.1, 0.5, (Q, 1))).astype(np.float32),
        "qs": (np.random.uniform(0.5, 2.0, (Q, 1)) * fq[:, None]).astype(np.float32),
        "msgs": (n((Q, E)) * 1 / np.sqrt(Q) / fq[:, None]).astype(np.float32),
        "old": (n((E, M)) * 1.0).astype(np.float32),
        "fade": (np.random.uniform(0.3, 0.9, (1, M))).astype(np.float32),
        "offs": striped(idx),
        "offs2": striped(idx2),
        "offs3": striped(idx3),
    }


def reference(query, keys_words, keys_scales, query2, notes, lam, qs, msgs, old, fade, offs, offs2, offs3):
    idx = unstriped(offs)
    idx2 = unstriped(offs2)
    idx3 = unstriped(offs3)
    keysu = unpack_weight(keys_words, keys_scales, "e4m3")
    queryq = mxq(f64(query), 0, "e4m3")
    keysidxg = keysu[:, idx]
    a = queryq.T @ keysidxg
    query2q = mxq(f64(query2), 0, "e4m3")
    notesidx2q = mxq(f64(notes)[:, idx2], 0, "e4m3")
    b = query2q.T @ notesidx2q
    s = np.maximum(a, b) + np.minimum(a, b) * f64(lam)
    w = sigmoid(s)
    wq = w * f64(qs)
    msgsq = mxq(f64(msgs), 0, "e4m3")
    wqq = mxq(wq, 0, "e4m3")
    dl = msgsq.T @ wqq
    df = np.zeros((E, M))
    df[:, idx3] = dl
    y = f64(old) * f64(fade) + df
    return y

@@ -1,0 +1,249 @@
+from contextlib import ExitStack
+
+import concourse.mybir as mybir
+from concourse.masks import make_identity
+
+D, T, I, Q, E, U, M = 512, 2048, 512, 512, 512, 1024, 1024
+FLOPS = 2 * (D * Q * I + D * Q * I + Q * E * I)
+
+F32 = mybir.dt.float32
+BF16 = mybir.dt.bfloat16
+I32 = mybir.dt.int32
+U32 = mybir.dt.uint32
+U16 = mybir.dt.uint16
+U8 = mybir.dt.uint8
+FP8X4 = mybir.dt.float8_e4m3fn_x4
+ALU = mybir.AluOpType
+ACT = mybir.ActivationFunctionType
+
+P = 128
+PACK = 4
+CHUNKS = 4
+W = I // CHUNKS
+LIST_COLS = W // 16
+
+
+def tile_attend_twopools_delivered_lean_kernel(
+    tc, query, keys_words, keys_scales, query2, notes, lam, qs, msgs, old, fade, offs, offs2, offs3, out
+):
+    nc = tc.nc
+    with ExitStack() as ctx:
+        keep = ctx.enter_context(tc.tile_pool(name="keep", bufs=1))
+        ring = ctx.enter_context(tc.tile_pool(name="ring", bufs=4))
+        psum = ctx.enter_context(tc.psum_pool(name="psum", bufs=1))
+
+        def quantise(name, grouped, width):
+            codes = keep.tile([P, width], U32, name=name + "_codes", align_bytes=64)
+            scales = keep.tile([P, width], U8, name=name + "_scales", align_bytes=64)
+            nc.vector.quantize_mx(out=codes[:].bitcast(FP8X4), scales=scales[:], in_=grouped)
+            return codes, scales
+
+        def products(bank, stationary, moving, mcols):
+            for r in range(4):
+                cols = slice(r * P, (r + 1) * P)
+                nc.tensor.matmul_mx(
+                    out=bank[:, r, :],
+                    lhsT=stationary[0][:, cols].bitcast(FP8X4),
+                    lhsT_scale=stationary[1][:, cols],
+                    rhs=moving[0][:, mcols].bitcast(FP8X4),
+                    rhs_scale=moving[1][:, mcols],
+                    start=True,
+                    stop=True,
+                )
+
+        def entries(list_tile, first, last):
+            return list_tile[:, first // 16 : last // 16]
+
+
+        key_bytes = keep.tile([P, T], U8, name="key_bytes", align_bytes=64)
+        nc.vector.memset(key_bytes[:].bitcast(I32), 0)
+        windows = [keep.tile([P, M], F32, name=f"window{k}") for k in range(4)]
+        for k in range(4):
+            nc.gpsimd.memset(windows[k][:], 0.0)
+
+        query2_raw = keep.tile([P, PACK, Q], F32, name="query2_raw")
+        query_raw = keep.tile([P, PACK, Q], F32, name="query_raw")
+        msgs_raw = keep.tile([P, PACK, E], F32, name="msgs_raw")
+        note_list = keep.tile([P, I // 16], U16, name="note_list")
+        key_list = keep.tile([P, I // 16], U16, name="key_list")
+        place_list = keep.tile([P, I // 16], U16, name="place_list")
+        note_planes = [keep.tile([P, U], F32, name=f"note_plane{j}") for j in range(PACK)]
+        key_words = keep.tile([P, T], U32, name="key_words")
+        lam_cols = keep.tile([P, PACK], F32, name="lam_cols")
+        qs_cols = keep.tile([P, PACK], F32, name="qs_cols")
+        fade_rows = keep.tile([P, P], F32, name="fade_rows")
+        nc.vector.memset(fade_rows[:], 0.0)
+        note_rows = notes.rearrange("(p j) u -> p j u", j=PACK)
+
+        def load_key_bytes(quad):
+            nc.sync.dma_start(
+                key_bytes[32 * quad : 32 * quad + 4, :].bitcast(I32),
+                keys_scales[0, 4 * quad : 4 * quad + 4, :].bitcast(I32),
+            )
+
+        nc.sync.dma_start(query2_raw[:], query2.rearrange("(p j) q -> p j q", j=PACK))
+        nc.sync.dma_start(note_list[:], offs2)
+        nc.sync.dma_start(note_planes[0][:], note_rows[:, 0, :])
+        nc.sync.dma_start(key_list[:], offs)
+        load_key_bytes(0)
+        for j in range(1, PACK):
+            load_key_bytes(j)
+            nc.sync.dma_start(note_planes[j][:], note_rows[:, j, :])
+        nc.sync.dma_start(query_raw[:], query.rearrange("(p j) q -> p j q", j=PACK))
+        nc.sync.dma_start(lam_cols[:], lam.rearrange("(p t) o -> p (t o)", t=PACK))
+        nc.sync.dma_start(
+            key_words[:].bitcast(I32), keys_words[0].rearrange("p n t -> p (n t)").bitcast(I32)
+        )
+        nc.sync.dma_start(msgs_raw[:], msgs.rearrange("(p j) e -> p j e", j=PACK))
+        nc.sync.dma_start(qs_cols[:], qs.rearrange("(p t) o -> p (t o)", t=PACK))
+        nc.sync.dma_start(place_list[:], offs3)
+        nc.sync.dma_start(fade_rows[0 : M // P, :], fade[0].rearrange("(c p) -> c p", p=P))
+        identity = keep.tile([P, P], F32, name="identity")
+        make_identity(nc, identity[:])
+        turned = psum.tile([P, P], F32, name="turned", tag="fade0")
+        nc.tensor.transpose(turned[:], fade_rows[:], identity[:])
+        fade_cols = keep.tile([P, M // P], F32, name="fade_cols")
+        nc.vector.tensor_copy(fade_cols[:], turned[:, 0 : M // P])
+        fade_banks = [psum.tile([P, 4, P], F32, name=f"fade_bank{h}", tag=f"fade{h}") for h in range(2)]
+        for c in range(M // P):
+            nc.tensor.transpose(
+                fade_banks[c // 4][:, c % 4, :], fade_cols[:, c : c + 1].to_broadcast([P, P]), identity[:]
+            )
+        olds = [keep.tile([P, M], F32, name=f"old{k}") for k in range(4)]
+        for k in range(4):
+            nc.sync.dma_start(olds[k][:], old[k * P : (k + 1) * P, :])
+
+        def deal(copy, grouped, raw, first, last):
+            copy(
+                out=grouped[:].rearrange("p t m j -> p m t j")[:, first:last],
+                in_=raw[:].rearrange("p j (m t) -> p m t j", t=PACK)[:, first:last],
+            )
+
+        query2_grouped = keep.tile([P, PACK, P, PACK], BF16, name="query2_grouped", align_bytes=64)
+        deal(nc.vector.tensor_copy, query2_grouped, query2_raw, 0, P)
+        query2_q = quantise("query2", query2_grouped[:].rearrange("p t m j -> p (t m j)"), Q)
+
+        picked_bytes = keep.tile([P, I], U8, name="picked_bytes", align_bytes=64)
+        nc.vector.tensor_copy(picked_bytes[:], key_bytes[:].indirect(key_list[:]))
+
+        picked = keep.tile([P, PACK, I], BF16, name="picked")
+        for j in range(PACK):
+            split = (I, 0, I, I // 4)[j]
+            if split > 0:
+                nc.scalar.activation(picked[:, j, :split], note_planes[j][:].indirect(entries(note_list, 0, split)), ACT.Copy)
+            if split < I:
+                nc.vector.tensor_copy(picked[:, j, split:], note_planes[j][:].indirect(entries(note_list, split, I)))
+        notes_grouped = keep.tile([P, I, PACK], BF16, name="notes_grouped", align_bytes=64)
+        nc.vector.tensor_copy(
+            out=notes_grouped[:].rearrange("p (c i) j -> p c j i", i=4),
+            in_=picked[:].rearrange("p j (c i) -> p c j i", i=4),
+        )
+        notes_q = quantise("notes", notes_grouped[:].rearrange("p i j -> p (i j)"), I)
+
+        query_grouped = keep.tile([P, PACK, P, PACK], BF16, name="query_grouped", align_bytes=64)
+        deal(nc.scalar.copy, query_grouped, query_raw, 0, P // 2)
+        deal(nc.vector.tensor_copy, query_grouped, query_raw, P // 2, P)
+        query_q = quantise("query", query_grouped[:].rearrange("p t m j -> p (t m j)"), Q)
+
+        b_sb = []
+        for chunk in range(CHUNKS):
+            bank = psum.tile([P, PACK, W], F32, name="b_bank", tag=f"low{chunk}")
+            products(bank, query2_q, notes_q, slice(chunk * W, (chunk + 1) * W))
+            b_chunk = keep.tile([P, PACK, W], F32, name=f"b{chunk}")
+            nc.scalar.copy(out=b_chunk[:], in_=bank[:])
+            b_sb.append(b_chunk)
+
+        picked_words = keep.tile([P, I], U32, name="picked_words", align_bytes=64)
+        keys_q = (picked_words, picked_bytes)
+
+        def pick_words(first, last):
+            nc.vector.tensor_copy(picked_words[:, first:last], key_words[:].indirect(entries(key_list, first, last)))
+
+        msgs_grouped = keep.tile([P, E, PACK], BF16, name="msgs_grouped", align_bytes=64)
+        nc.scalar.copy(
+            out=msgs_grouped[:].rearrange("p (c i) j -> p c j i", i=4),
+            in_=msgs_raw[:].rearrange("p j (c i) -> p c j i", i=4),
+        )
+
+        weights = []
+
+        def score(chunk):
+            pick_words(chunk * W, (chunk + 1) * W)
+            larger = ring.tile([P, PACK, W], F32, name="larger")
+            smaller = keep.tile([P, PACK, W], F32, name="smaller", tag=f"shared{chunk % 2}")
+            bank = psum.tile([P, PACK, W], F32, name="a_bank", tag=f"high{chunk % 2}")
+            products(bank, query_q, keys_q, slice(chunk * W, (chunk + 1) * W))
+            nc.vector.tensor_tensor(smaller[:], bank[:], b_sb[chunk][:], ALU.min)
+            nc.vector.tensor_tensor(larger[:], bank[:], b_sb[chunk][:], ALU.max)
+            scores = ring.tile([P, PACK, W], F32, name="scores")
+            for t in range(PACK):
+                nc.vector.scalar_tensor_tensor(
+                    scores[:, t, :], smaller[:, t, :], lam_cols[:, t : t + 1], larger[:, t, :], ALU.mult, ALU.add
+                )
+            w = keep.tile([P, W, PACK], F32, name="w", tag=f"shared{chunk % 2}")
+            nc.scalar.activation(w[:], scores[:].rearrange("p t i -> p i t"), ACT.Sigmoid)
+            weights.append(w)
+
+        dl_banks = []
+
+        def weigh(chunk):
+            wq = ring.tile([P, W, PACK], BF16, name="wq", align_bytes=64)
+            nc.vector.tensor_tensor(
+                wq[:], weights[chunk][:], qs_cols[:].unsqueeze(1).to_broadcast([P, W, PACK]), ALU.mult
+            )
+            wq_q = quantise(f"wq{chunk}", wq[:].rearrange("p i t -> p (i t)"), W)
+            bank = psum.tile([P, 4, W], F32, name="dl_bank", tag=f"low{chunk}")
+            products(bank, msgs_q, wq_q, slice(0, W))
+            dl_banks.append(bank)
+
+        dl = keep.tile([P, 4, I], F32, name="dl")
+
+        def empty(chunk, copy):
+            copy(out=dl[:, :, chunk * W : (chunk + 1) * W], in_=dl_banks[chunk][:])
+
+        def scatter(k, first, last, on_vector):
+            window = windows[k][:].indirect(entries(place_list, first, last))
+            if on_vector:
+                nc.vector.tensor_copy(window, dl[:, k, first:last])
+            else:
+                nc.scalar.activation(window, dl[:, k, first:last], ACT.Copy)
+
+        def finish(k, first, last, engine):
+            engine.tensor_tensor(olds[k][:, first:last], olds[k][:, first:last], windows[k][:, first:last], ALU.add)
+            nc.sync.dma_start(out[k * P : (k + 1) * P, first:last], olds[k][:, first:last])
+
+        def faded(k):
+            for h in range(2):
+                cols = slice(h * 512, (h + 1) * 512)
+                nc.vector.tensor_tensor(
+                    olds[k][:, cols], olds[k][:, cols], fade_banks[h][:].rearrange("p c m -> p (c m)"), ALU.mult
+                )
+
+        score(0)
+        score(1)
+        msgs_q = quantise("msgs", msgs_grouped[:].rearrange("p e j -> p (e j)"), E)
+        for chunk in range(CHUNKS):
+            weigh(chunk)
+            empty(chunk, [nc.scalar.copy, nc.scalar.copy, nc.scalar.copy, nc.vector.tensor_copy][chunk])
+            if chunk + 2 < CHUNKS:
+                score(chunk + 2)
+        for k in range(4):
+            scatter(k, 0, W, False)
+        for k in range(3):
+            scatter(k, W, 2 * W, False)
+        scatter(0, 2 * W, 3 * W, False)
+        scatter(1, 2 * W, 3 * W, False)
+        scatter(3, W, 3 * W, False)
+        faded(0)
+        scatter(0, 3 * W, I, False)
+        finish(0, 0, M, nc.vector)
+        faded(1)
+        scatter(1, 3 * W, I, False)
+        finish(1, 0, M, nc.vector)
+        faded(3)
+        faded(2)
+        scatter(3, 3 * W, I, False)
+        finish(3, 0, M, nc.vector)
+        scatter(2, 2 * W, I, False)
+        finish(2, 0, M // 2, nc.vector)
+        finish(2, M // 2, M, nc.vector)

@@ -32,6 +32,9 @@ def tile_attend_twopools_delivered_lean_kernel(
         ring = ctx.enter_context(tc.tile_pool(name="ring", bufs=4))
         psum = ctx.enter_context(tc.psum_pool(name="psum", bufs=1))
 
+        key_bytes = keep.tile([P, T], U8, name="key_bytes", align_bytes=64)
+        nc.gpsimd.memset(key_bytes[:].bitcast(I32), 0)
+
         def quantise(name, grouped, width):
             codes = keep.tile([P, width], U32, name=name + "_codes", align_bytes=64)
             scales = keep.tile([P, width], U8, name=name + "_scales", align_bytes=64)
@@ -54,16 +57,17 @@ def tile_attend_twopools_delivered_lean_kernel(
         def entries(list_tile, first, last):
             return list_tile[:, first // 16 : last // 16]
 
+        warm = keep.tile([P, 8], F32, name="warm")
+        nc.gpsimd.memset(warm[:], 0.0)
+        nc.scalar.activation(warm[:, 0:1], warm[:, 4:5], ACT.Sigmoid)
 
-        key_bytes = keep.tile([P, T], U8, name="key_bytes", align_bytes=64)
-        nc.vector.memset(key_bytes[:].bitcast(I32), 0)
         windows = [keep.tile([P, M], F32, name=f"window{k}") for k in range(4)]
         for k in range(4):
-            nc.gpsimd.memset(windows[k][:], 0.0)
+            (nc.vector if k < 2 else nc.gpsimd).memset(windows[k][:], 0.0)
 
         query2_raw = keep.tile([P, PACK, Q], F32, name="query2_raw")
-        query_raw = keep.tile([P, PACK, Q], F32, name="query_raw")
-        msgs_raw = keep.tile([P, PACK, E], F32, name="msgs_raw")
+        query_raw = [keep.tile([P, PACK, Q // 2], F32, name=f"query_raw{h}") for h in range(2)]
+        msgs_raw = [keep.tile([P, PACK, E // 2], F32, name=f"msgs_raw{h}") for h in range(2)]
         note_list = keep.tile([P, I // 16], U16, name="note_list")
         key_list = keep.tile([P, I // 16], U16, name="key_list")
         place_list = keep.tile([P, I // 16], U16, name="place_list")
@@ -77,8 +81,8 @@ def tile_attend_twopools_delivered_lean_kernel(
 
         def load_key_bytes(quad):
             nc.sync.dma_start(
-                key_bytes[32 * quad : 32 * quad + 4, :].bitcast(I32),
-                keys_scales[0, 4 * quad : 4 * quad + 4, :].bitcast(I32),
+                key_bytes[quad : P : 32, :].bitcast(I32),
+                keys_scales[0, quad : 16 : 4, :].bitcast(I32),
             )
 
         nc.sync.dma_start(query2_raw[:], query2.rearrange("(p j) q -> p j q", j=PACK))
@@ -89,26 +93,21 @@ def tile_attend_twopools_delivered_lean_kernel(
         for j in range(1, PACK):
             load_key_bytes(j)
             nc.sync.dma_start(note_planes[j][:], note_rows[:, j, :])
-        nc.sync.dma_start(query_raw[:], query.rearrange("(p j) q -> p j q", j=PACK))
-        nc.sync.dma_start(lam_cols[:], lam.rearrange("(p t) o -> p (t o)", t=PACK))
+        query_rows = query.rearrange("(p j) q -> p j q", j=PACK)
+        for h in range(2):
+            nc.sync.dma_start(query_raw[h][:], query_rows[:, :, h * Q // 2 : (h + 1) * Q // 2])
         nc.sync.dma_start(
             key_words[:].bitcast(I32), keys_words[0].rearrange("p n t -> p (n t)").bitcast(I32)
         )
-        nc.sync.dma_start(msgs_raw[:], msgs.rearrange("(p j) e -> p j e", j=PACK))
+        nc.sync.dma_start(lam_cols[:], lam.rearrange("(p t) o -> p (t o)", t=PACK))
+        msgs_rows = msgs.rearrange("(p j) e -> p j e", j=PACK)
+        for h in range(2):
+            nc.sync.dma_start(msgs_raw[h][:], msgs_rows[:, :, h * E // 2 : (h + 1) * E // 2])
         nc.sync.dma_start(qs_cols[:], qs.rearrange("(p t) o -> p (t o)", t=PACK))
         nc.sync.dma_start(place_list[:], offs3)
         nc.sync.dma_start(fade_rows[0 : M // P, :], fade[0].rearrange("(c p) -> c p", p=P))
         identity = keep.tile([P, P], F32, name="identity")
         make_identity(nc, identity[:])
-        turned = psum.tile([P, P], F32, name="turned", tag="fade0")
-        nc.tensor.transpose(turned[:], fade_rows[:], identity[:])
-        fade_cols = keep.tile([P, M // P], F32, name="fade_cols")
-        nc.vector.tensor_copy(fade_cols[:], turned[:, 0 : M // P])
-        fade_banks = [psum.tile([P, 4, P], F32, name=f"fade_bank{h}", tag=f"fade{h}") for h in range(2)]
-        for c in range(M // P):
-            nc.tensor.transpose(
-                fade_banks[c // 4][:, c % 4, :], fade_cols[:, c : c + 1].to_broadcast([P, P]), identity[:]
-            )
         olds = [keep.tile([P, M], F32, name=f"old{k}") for k in range(4)]
         for k in range(4):
             nc.sync.dma_start(olds[k][:], old[k * P : (k + 1) * P, :])
@@ -116,7 +115,7 @@ def tile_attend_twopools_delivered_lean_kernel(
         def deal(copy, grouped, raw, first, last):
             copy(
                 out=grouped[:].rearrange("p t m j -> p m t j")[:, first:last],
-                in_=raw[:].rearrange("p j (m t) -> p m t j", t=PACK)[:, first:last],
+                in_=raw[:].rearrange("p j (m t) -> p m t j", t=PACK),
             )
 
         query2_grouped = keep.tile([P, PACK, P, PACK], BF16, name="query2_grouped", align_bytes=64)
@@ -140,54 +139,59 @@ def tile_attend_twopools_delivered_lean_kernel(
         )
         notes_q = quantise("notes", notes_grouped[:].rearrange("p i j -> p (i j)"), I)
 
-        query_grouped = keep.tile([P, PACK, P, PACK], BF16, name="query_grouped", align_bytes=64)
-        deal(nc.scalar.copy, query_grouped, query_raw, 0, P // 2)
-        deal(nc.vector.tensor_copy, query_grouped, query_raw, P // 2, P)
-        query_q = quantise("query", query_grouped[:].rearrange("p t m j -> p (t m j)"), Q)
-
-        b_sb = []
-        for chunk in range(CHUNKS):
-            bank = psum.tile([P, PACK, W], F32, name="b_bank", tag=f"low{chunk}")
-            products(bank, query2_q, notes_q, slice(chunk * W, (chunk + 1) * W))
-            b_chunk = keep.tile([P, PACK, W], F32, name=f"b{chunk}")
-            nc.scalar.copy(out=b_chunk[:], in_=bank[:])
-            b_sb.append(b_chunk)
-
         picked_words = keep.tile([P, I], U32, name="picked_words", align_bytes=64)
         keys_q = (picked_words, picked_bytes)
+
+        query_grouped = keep.tile([P, PACK, P, PACK], BF16, name="query_grouped", align_bytes=64)
+        deal(nc.scalar.copy, query_grouped, query_raw[0], 0, P // 2)
+        deal(nc.vector.tensor_copy, query_grouped, query_raw[1], P // 2, P)
+        query_q = quantise("query", query_grouped[:].rearrange("p t m j -> p (t m j)"), Q)
 
         def pick_words(first, last):
             nc.vector.tensor_copy(picked_words[:, first:last], key_words[:].indirect(entries(key_list, first, last)))
 
+        b_sb = []
+
+        def empty_b(chunk):
+            bank = psum.tile([P, PACK, W], F32, name="b_bank", tag=f"low{chunk}")
+            products(bank, query2_q, notes_q, slice(chunk * W, (chunk + 1) * W))
+            b_chunk = keep.tile([P, PACK, W], F32, name="b_chunk", tag=["b0", "b1", "msgs_raw1", "scores0"][chunk])
+            nc.scalar.copy(out=b_chunk[:], in_=bank[:])
+            b_sb.append(b_chunk)
+
+        empty_b(0)
+
         msgs_grouped = keep.tile([P, E, PACK], BF16, name="msgs_grouped", align_bytes=64)
-        nc.scalar.copy(
-            out=msgs_grouped[:].rearrange("p (c i) j -> p c j i", i=4),
-            in_=msgs_raw[:].rearrange("p j (c i) -> p c j i", i=4),
-        )
+        for h in range(2):
+            nc.scalar.copy(
+                out=msgs_grouped[:, h * E // 2 : (h + 1) * E // 2, :].rearrange("p (c i) j -> p c j i", i=4),
+                in_=msgs_raw[h][:].rearrange("p j (c i) -> p c j i", i=4),
+            )
 
         weights = []
 
         def score(chunk):
-            pick_words(chunk * W, (chunk + 1) * W)
-            larger = ring.tile([P, PACK, W], F32, name="larger")
-            smaller = keep.tile([P, PACK, W], F32, name="smaller", tag=f"shared{chunk % 2}")
-            bank = psum.tile([P, PACK, W], F32, name="a_bank", tag=f"high{chunk % 2}")
+            if chunk >= 1:
+                empty_b(chunk)
+            both = keep.tile([P, 2, PACK, W], F32, name="both", tag=["x0","r1","r1","r1"][chunk], align_bytes=64)
+            smaller, larger = both[:, 0], both[:, 1]
+            bank = psum.tile([P, PACK, W], F32, name="a_bank", tag=f"high{chunk}")
             products(bank, query_q, keys_q, slice(chunk * W, (chunk + 1) * W))
-            nc.vector.tensor_tensor(smaller[:], bank[:], b_sb[chunk][:], ALU.min)
-            nc.vector.tensor_tensor(larger[:], bank[:], b_sb[chunk][:], ALU.max)
-            scores = ring.tile([P, PACK, W], F32, name="scores")
+            nc.vector.tensor_tensor(smaller, bank[:], b_sb[chunk][:], ALU.min)
+            nc.vector.tensor_tensor(larger, bank[:], b_sb[chunk][:], ALU.max)
+            scores = keep.tile([P, PACK, W], F32, name=f"scores{chunk}")
             for t in range(PACK):
                 nc.vector.scalar_tensor_tensor(
                     scores[:, t, :], smaller[:, t, :], lam_cols[:, t : t + 1], larger[:, t, :], ALU.mult, ALU.add
                 )
-            w = keep.tile([P, W, PACK], F32, name="w", tag=f"shared{chunk % 2}")
+            w = keep.tile([P, W, PACK], F32, name="w", tag=["r1","w1","w2","w3"][chunk], align_bytes=64)
             nc.scalar.activation(w[:], scores[:].rearrange("p t i -> p i t"), ACT.Sigmoid)
             weights.append(w)
 
         dl_banks = []
 
         def weigh(chunk):
-            wq = ring.tile([P, W, PACK], BF16, name="wq", align_bytes=64)
+            wq = keep.tile([P, W, PACK], BF16, name="wq", tag=["q0","q1","q2","q3"][chunk], align_bytes=64)
             nc.vector.tensor_tensor(
                 wq[:], weights[chunk][:], qs_cols[:].unsqueeze(1).to_broadcast([P, W, PACK]), ALU.mult
             )
@@ -198,15 +202,16 @@ def tile_attend_twopools_delivered_lean_kernel(
 
         dl = keep.tile([P, 4, I], F32, name="dl")
 
-        def empty(chunk, copy):
-            copy(out=dl[:, :, chunk * W : (chunk + 1) * W], in_=dl_banks[chunk][:])
+        def empty(chunk, copy, first=0, last=4):
+            copy(out=dl[:, first:last, chunk * W : (chunk + 1) * W], in_=dl_banks[chunk][:, first:last, :])
 
         def scatter(k, first, last, on_vector):
             window = windows[k][:].indirect(entries(place_list, first, last))
+            source = dl[:, k, first:last]
             if on_vector:
-                nc.vector.tensor_copy(window, dl[:, k, first:last])
+                nc.vector.tensor_copy(window, source)
             else:
-                nc.scalar.activation(window, dl[:, k, first:last], ACT.Copy)
+                nc.scalar.activation(window, source, ACT.Copy)
 
         def finish(k, first, last, engine):
             engine.tensor_tensor(olds[k][:, first:last], olds[k][:, first:last], windows[k][:, first:last], ALU.add)
@@ -219,31 +224,54 @@ def tile_attend_twopools_delivered_lean_kernel(
                     olds[k][:, cols], olds[k][:, cols], fade_banks[h][:].rearrange("p c m -> p (c m)"), ALU.mult
                 )
 
+        pick_words(0 * W, 1 * W)
         score(0)
-        score(1)
+        pick_words(1 * W, 4 * W)
         msgs_q = quantise("msgs", msgs_grouped[:].rearrange("p e j -> p (e j)"), E)
-        for chunk in range(CHUNKS):
-            weigh(chunk)
-            empty(chunk, [nc.scalar.copy, nc.scalar.copy, nc.scalar.copy, nc.vector.tensor_copy][chunk])
-            if chunk + 2 < CHUNKS:
-                score(chunk + 2)
-        for k in range(4):
-            scatter(k, 0, W, False)
-        for k in range(3):
-            scatter(k, W, 2 * W, False)
+        weigh(0)
+        empty(0, nc.scalar.copy, 0, 2)
+        score(1)
+        empty(0, nc.vector.tensor_copy, 2, 4)
+        weigh(1)
+        score(2)
+        empty(1, nc.scalar.copy, 0, 4)
+        weigh(2)
+        score(3)
+        empty(2, nc.vector.tensor_copy, 0, 4)
+        weigh(3)
+        empty(3, nc.scalar.copy, 0, 4)
+        turned = psum.tile([P, P], F32, name="turned", tag="high0")
+        nc.tensor.transpose(turned[:], fade_rows[:], identity[:])
+        fade_cols = keep.tile([P, M // P], F32, name="fade_cols")
+        nc.vector.tensor_copy(fade_cols[:], turned[:, 0 : M // P])
+        fade_banks = [psum.tile([P, 4, P], F32, name=f"fade_bank{h}", tag=f"high{h + 2}") for h in range(2)]
+        for c in range(M // P):
+            nc.tensor.transpose(
+                fade_banks[c // 4][:, c % 4, :], fade_cols[:, c : c + 1].to_broadcast([P, P]), identity[:]
+            )
+        scatter(0, 0 * W, 1 * W, False)
+        scatter(1, 0 * W, 1 * W, False)
+        scatter(2, 0 * W, 1 * W, False)
+        scatter(3, 0 * W, 1 * W, False)
+        scatter(0, 1 * W, 2 * W, False)
+        scatter(1, 1 * W, 2 * W, False)
+        scatter(2, 1 * W, 2 * W, False)
         scatter(0, 2 * W, 3 * W, False)
         scatter(1, 2 * W, 3 * W, False)
-        scatter(3, W, 3 * W, False)
+        scatter(2, 2 * W, 3 * W, False)
         faded(0)
-        scatter(0, 3 * W, I, False)
-        finish(0, 0, M, nc.vector)
         faded(1)
-        scatter(1, 3 * W, I, False)
-        finish(1, 0, M, nc.vector)
-        faded(3)
         faded(2)
-        scatter(3, 3 * W, I, False)
-        finish(3, 0, M, nc.vector)
-        scatter(2, 2 * W, I, False)
+        faded(3)
+        scatter(0, 3 * W, 4 * W, False)
+        finish(0, 0, M // 2, nc.vector)
+        finish(0, M // 2, M, nc.vector)
+        scatter(1, 3 * W, 4 * W, False)
+        finish(1, 0, M // 2, nc.vector)
+        finish(1, M // 2, M, nc.vector)
+        scatter(2, 3 * W, 4 * W, False)
         finish(2, 0, M // 2, nc.vector)
         finish(2, M // 2, M, nc.vector)
+        scatter(3, 1 * W, 4 * W, False)
+        finish(3, 0, M // 2, nc.vector)
+        finish(3, M // 2, M, nc.vector)

@@ -18,9 +18,18 @@ ACT = mybir.ActivationFunctionType
 
 P = 128
 PACK = 4
+LIST_ROWS = 16
+QUADRANT = 32
+ALIGN = 64
 CHUNKS = 4
 W = I // CHUNKS
-LIST_COLS = W // 16
+ROW_TILES = E // P
+LAST = ROW_TILES - 1
+HALF = M // 2
+
+SCALAR_NOTE_ENTRIES = (I, 0, I, I // 4)
+SCALAR_NOTE_SLOTS = 160
+SCALAR_QUERY_ROWS = P // 2
 
 
 def tile_attend_twopools_delivered_lean_kernel(
@@ -28,250 +37,240 @@ def tile_attend_twopools_delivered_lean_kernel(
 ):
     nc = tc.nc
     with ExitStack() as ctx:
-        keep = ctx.enter_context(tc.tile_pool(name="keep", bufs=1))
-        ring = ctx.enter_context(tc.tile_pool(name="ring", bufs=4))
+        sbuf = ctx.enter_context(tc.tile_pool(name="sbuf", bufs=1))
         psum = ctx.enter_context(tc.psum_pool(name="psum", bufs=1))
 
-        key_bytes = keep.tile([P, T], U8, name="key_bytes", align_bytes=64)
-        nc.gpsimd.memset(key_bytes[:].bitcast(I32), 0)
-
         def quantise(name, grouped, width):
-            codes = keep.tile([P, width], U32, name=name + "_codes", align_bytes=64)
-            scales = keep.tile([P, width], U8, name=name + "_scales", align_bytes=64)
+            codes = sbuf.tile([P, width], U32, name=name + "_codes", align_bytes=ALIGN)
+            scales = sbuf.tile([P, width], U8, name=name + "_scales", align_bytes=ALIGN)
             nc.vector.quantize_mx(out=codes[:].bitcast(FP8X4), scales=scales[:], in_=grouped)
             return codes, scales
 
-        def products(bank, stationary, moving, mcols):
-            for r in range(4):
+        def products(bank, stationary, moving, moving_cols):
+            for r in range(bank.shape[1]):
                 cols = slice(r * P, (r + 1) * P)
                 nc.tensor.matmul_mx(
                     out=bank[:, r, :],
                     lhsT=stationary[0][:, cols].bitcast(FP8X4),
                     lhsT_scale=stationary[1][:, cols],
-                    rhs=moving[0][:, mcols].bitcast(FP8X4),
-                    rhs_scale=moving[1][:, mcols],
+                    rhs=moving[0][:, moving_cols].bitcast(FP8X4),
+                    rhs_scale=moving[1][:, moving_cols],
                     start=True,
                     stop=True,
                 )
 
         def entries(list_tile, first, last):
-            return list_tile[:, first // 16 : last // 16]
+            return list_tile[:, first // LIST_ROWS : last // LIST_ROWS]
 
-        warm = keep.tile([P, 8], F32, name="warm")
-        nc.gpsimd.memset(warm[:], 0.0)
-        nc.scalar.activation(warm[:, 0:1], warm[:, 4:5], ACT.Sigmoid)
+        def slots(chunk):
+            return slice(chunk * W, (chunk + 1) * W)
 
-        windows = [keep.tile([P, M], F32, name=f"window{k}") for k in range(4)]
-        for k in range(4):
-            (nc.vector if k < 2 else nc.gpsimd).memset(windows[k][:], 0.0)
+        key_bytes = sbuf.tile([P, T], U8, name="key_bytes", align_bytes=ALIGN)
+        nc.gpsimd.memset(key_bytes[:].bitcast(I32), 0)
 
-        query2_raw = keep.tile([P, PACK, Q], F32, name="query2_raw")
-        query_raw = [keep.tile([P, PACK, Q // 2], F32, name=f"query_raw{h}") for h in range(2)]
-        msgs_raw = [keep.tile([P, PACK, E // 2], F32, name=f"msgs_raw{h}") for h in range(2)]
-        note_list = keep.tile([P, I // 16], U16, name="note_list")
-        key_list = keep.tile([P, I // 16], U16, name="key_list")
-        place_list = keep.tile([P, I // 16], U16, name="place_list")
-        note_planes = [keep.tile([P, U], F32, name=f"note_plane{j}") for j in range(PACK)]
-        key_words = keep.tile([P, T], U32, name="key_words")
-        lam_cols = keep.tile([P, PACK], F32, name="lam_cols")
-        qs_cols = keep.tile([P, PACK], F32, name="qs_cols")
-        fade_rows = keep.tile([P, P], F32, name="fade_rows")
+        warm_in = sbuf.tile([P, 1], F32, name="warm_in")
+        warm_out = sbuf.tile([P, 1], F32, name="warm_out")
+        nc.gpsimd.memset(warm_in[:], 0.0)
+        nc.scalar.activation(warm_out[:], warm_in[:], ACT.Sigmoid)
+
+        delivered = [sbuf.tile([P, M], F32, name=f"delivered{k}") for k in range(ROW_TILES)]
+        for k in range(ROW_TILES):
+            (nc.vector if k < ROW_TILES // 2 else nc.gpsimd).memset(delivered[k][:], 0.0)
+        fade_rows = sbuf.tile([P, P], F32, name="fade_rows")
         nc.vector.memset(fade_rows[:], 0.0)
-        note_rows = notes.rearrange("(p j) u -> p j u", j=PACK)
 
-        def load_key_bytes(quad):
-            nc.sync.dma_start(
-                key_bytes[quad : P : 32, :].bitcast(I32),
-                keys_scales[0, quad : 16 : 4, :].bitcast(I32),
-            )
-
+        query2_raw = sbuf.tile([P, PACK, Q], F32, name="query2_raw")
         nc.sync.dma_start(query2_raw[:], query2.rearrange("(p j) q -> p j q", j=PACK))
+        note_list = sbuf.tile([P, I // LIST_ROWS], U16, name="note_list")
         nc.sync.dma_start(note_list[:], offs2)
+        note_rows = notes.rearrange("(p j) u -> p j u", j=PACK)
+        note_planes = [sbuf.tile([P, U], F32, name=f"note_plane{j}") for j in range(PACK)]
+        key_list = sbuf.tile([P, I // LIST_ROWS], U16, name="key_list")
         nc.sync.dma_start(note_planes[0][:], note_rows[:, 0, :])
         nc.sync.dma_start(key_list[:], offs)
-        load_key_bytes(0)
-        for j in range(1, PACK):
-            load_key_bytes(j)
-            nc.sync.dma_start(note_planes[j][:], note_rows[:, j, :])
-        query_rows = query.rearrange("(p j) q -> p j q", j=PACK)
-        for h in range(2):
-            nc.sync.dma_start(query_raw[h][:], query_rows[:, :, h * Q // 2 : (h + 1) * Q // 2])
-        nc.sync.dma_start(
-            key_words[:].bitcast(I32), keys_words[0].rearrange("p n t -> p (n t)").bitcast(I32)
-        )
+        for j in range(PACK):
+            nc.sync.dma_start(
+                key_bytes[j:P:QUADRANT, :].bitcast(I32), keys_scales[0, j : D // 32 : PACK, :].bitcast(I32)
+            )
+            if j > 0:
+                nc.sync.dma_start(note_planes[j][:], note_rows[:, j, :])
+        query_raw = sbuf.tile([P, PACK, Q], F32, name="query_raw")
+        nc.sync.dma_start(query_raw[:], query.rearrange("(p j) q -> p j q", j=PACK))
+        key_words = sbuf.tile([P, T], U32, name="key_words")
+        nc.sync.dma_start(key_words[:].bitcast(I32), keys_words[0].rearrange("p n t -> p (n t)").bitcast(I32))
+        lam_cols = sbuf.tile([P, PACK], F32, name="lam_cols")
         nc.sync.dma_start(lam_cols[:], lam.rearrange("(p t) o -> p (t o)", t=PACK))
         msgs_rows = msgs.rearrange("(p j) e -> p j e", j=PACK)
-        for h in range(2):
-            nc.sync.dma_start(msgs_raw[h][:], msgs_rows[:, :, h * E // 2 : (h + 1) * E // 2])
+        msgs_halves = [slice(0, E // 2), slice(E // 2, E)]
+        msgs_raw = []
+        for cols, tag in zip(msgs_halves, ("msgs_first", "chain")):
+            raw = sbuf.tile([P, PACK, E // 2], F32, name="msgs_raw", tag=tag, align_bytes=ALIGN)
+            nc.sync.dma_start(raw[:], msgs_rows[:, :, cols])
+            msgs_raw.append(raw)
+        qs_cols = sbuf.tile([P, PACK], F32, name="qs_cols")
         nc.sync.dma_start(qs_cols[:], qs.rearrange("(p t) o -> p (t o)", t=PACK))
+        place_list = sbuf.tile([P, I // LIST_ROWS], U16, name="place_list")
         nc.sync.dma_start(place_list[:], offs3)
         nc.sync.dma_start(fade_rows[0 : M // P, :], fade[0].rearrange("(c p) -> c p", p=P))
-        identity = keep.tile([P, P], F32, name="identity")
+        identity = sbuf.tile([P, P], F32, name="identity")
         make_identity(nc, identity[:])
-        olds = [keep.tile([P, M], F32, name=f"old{k}") for k in range(4)]
-        for k in range(4):
-            nc.sync.dma_start(olds[k][:], old[k * P : (k + 1) * P, :])
+        results = [sbuf.tile([P, M], F32, name=f"result{k}") for k in range(ROW_TILES)]
+        for k in range(ROW_TILES):
+            nc.sync.dma_start(results[k][:], old[k * P : (k + 1) * P, :])
 
         def deal(copy, grouped, raw, first, last):
             copy(
                 out=grouped[:].rearrange("p t m j -> p m t j")[:, first:last],
-                in_=raw[:].rearrange("p j (m t) -> p m t j", t=PACK),
+                in_=raw[:].rearrange("p j (m t) -> p m t j", t=PACK)[:, first:last],
             )
 
-        query2_grouped = keep.tile([P, PACK, P, PACK], BF16, name="query2_grouped", align_bytes=64)
+        def interleave(copy, grouped, planes):
+            copy(
+                out=grouped.rearrange("p (c i) j -> p c j i", i=PACK),
+                in_=planes.rearrange("p j (c i) -> p c j i", i=PACK),
+            )
+
+        query2_grouped = sbuf.tile([P, PACK, P, PACK], BF16, name="query2_grouped", align_bytes=ALIGN)
         deal(nc.vector.tensor_copy, query2_grouped, query2_raw, 0, P)
         query2_q = quantise("query2", query2_grouped[:].rearrange("p t m j -> p (t m j)"), Q)
 
-        picked_bytes = keep.tile([P, I], U8, name="picked_bytes", align_bytes=64)
+        picked_bytes = sbuf.tile([P, I], U8, name="picked_bytes", align_bytes=ALIGN)
         nc.vector.tensor_copy(picked_bytes[:], key_bytes[:].indirect(key_list[:]))
 
-        picked = keep.tile([P, PACK, I], BF16, name="picked")
-        for j in range(PACK):
-            split = (I, 0, I, I // 4)[j]
+        picked_notes = sbuf.tile([P, PACK, I], BF16, name="picked_notes")
+        for j, split in enumerate(SCALAR_NOTE_ENTRIES):
             if split > 0:
-                nc.scalar.activation(picked[:, j, :split], note_planes[j][:].indirect(entries(note_list, 0, split)), ACT.Copy)
+                window = note_planes[j][:].indirect(entries(note_list, 0, split))
+                nc.scalar.activation(picked_notes[:, j, :split], window, ACT.Copy)
             if split < I:
-                nc.vector.tensor_copy(picked[:, j, split:], note_planes[j][:].indirect(entries(note_list, split, I)))
-        notes_grouped = keep.tile([P, I, PACK], BF16, name="notes_grouped", align_bytes=64)
-        nc.vector.tensor_copy(
-            out=notes_grouped[:].rearrange("p (c i) j -> p c j i", i=4),
-            in_=picked[:].rearrange("p j (c i) -> p c j i", i=4),
-        )
+                window = note_planes[j][:].indirect(entries(note_list, split, I))
+                nc.vector.tensor_copy(picked_notes[:, j, split:], window)
+        notes_grouped = sbuf.tile([P, I, PACK], BF16, name="notes_grouped", align_bytes=ALIGN)
+        for copy, cols in (
+            (nc.scalar.copy, slice(0, SCALAR_NOTE_SLOTS)),
+            (nc.vector.tensor_copy, slice(SCALAR_NOTE_SLOTS, I)),
+        ):
+            interleave(copy, notes_grouped[:, cols, :], picked_notes[:, :, cols])
         notes_q = quantise("notes", notes_grouped[:].rearrange("p i j -> p (i j)"), I)
 
-        picked_words = keep.tile([P, I], U32, name="picked_words", align_bytes=64)
-        keys_q = (picked_words, picked_bytes)
-
-        query_grouped = keep.tile([P, PACK, P, PACK], BF16, name="query_grouped", align_bytes=64)
-        deal(nc.scalar.copy, query_grouped, query_raw[0], 0, P // 2)
-        deal(nc.vector.tensor_copy, query_grouped, query_raw[1], P // 2, P)
+        query_grouped = sbuf.tile([P, PACK, P, PACK], BF16, name="query_grouped", align_bytes=ALIGN)
+        deal(nc.scalar.copy, query_grouped, query_raw, 0, SCALAR_QUERY_ROWS)
+        deal(nc.vector.tensor_copy, query_grouped, query_raw, SCALAR_QUERY_ROWS, P)
         query_q = quantise("query", query_grouped[:].rearrange("p t m j -> p (t m j)"), Q)
+
+        picked_words = sbuf.tile([P, I], U32, name="picked_words", align_bytes=ALIGN)
+        keys_q = (picked_words, picked_bytes)
 
         def pick_words(first, last):
             nc.vector.tensor_copy(picked_words[:, first:last], key_words[:].indirect(entries(key_list, first, last)))
 
-        b_sb = []
+        b_tags = ("b0", "b1", "scores0", "msgs_grouped")
+        b_bank_tags = ("dl0", "dl1", "a0", "dl3")
+        b_chunks, weights, dl_banks, sums = [], [], [], {}
 
-        def empty_b(chunk):
-            bank = psum.tile([P, PACK, W], F32, name="b_bank", tag=f"low{chunk}")
-            products(bank, query2_q, notes_q, slice(chunk * W, (chunk + 1) * W))
-            b_chunk = keep.tile([P, PACK, W], F32, name="b_chunk", tag=["b0", "b1", "msgs_raw1", "scores0"][chunk])
+        def second_scores(chunk):
+            bank = psum.tile([P, PACK, W], F32, name="b_bank", tag=b_bank_tags[chunk])
+            products(bank, query2_q, notes_q, slots(chunk))
+            b_chunk = sbuf.tile([P, PACK, W], F32, name="b_chunk", tag=b_tags[chunk], align_bytes=ALIGN)
             nc.scalar.copy(out=b_chunk[:], in_=bank[:])
-            b_sb.append(b_chunk)
-
-        empty_b(0)
-
-        msgs_grouped = keep.tile([P, E, PACK], BF16, name="msgs_grouped", align_bytes=64)
-        for h in range(2):
-            nc.scalar.copy(
-                out=msgs_grouped[:, h * E // 2 : (h + 1) * E // 2, :].rearrange("p (c i) j -> p c j i", i=4),
-                in_=msgs_raw[h][:].rearrange("p j (c i) -> p c j i", i=4),
-            )
-
-        weights = []
+            b_chunks.append(b_chunk)
 
         def score(chunk):
-            if chunk >= 1:
-                empty_b(chunk)
-            both = keep.tile([P, 2, PACK, W], F32, name="both", tag=["x0","r1","r1","r1"][chunk], align_bytes=64)
-            smaller, larger = both[:, 0], both[:, 1]
-            bank = psum.tile([P, PACK, W], F32, name="a_bank", tag=f"high{chunk}")
-            products(bank, query_q, keys_q, slice(chunk * W, (chunk + 1) * W))
-            nc.vector.tensor_tensor(smaller, bank[:], b_sb[chunk][:], ALU.min)
-            nc.vector.tensor_tensor(larger, bank[:], b_sb[chunk][:], ALU.max)
-            scores = keep.tile([P, PACK, W], F32, name=f"scores{chunk}")
+            extremes_tag = "chain" if chunk > 0 else "extremes0"
+            extremes = sbuf.tile([P, 2, PACK, W], F32, name="extremes", tag=extremes_tag, align_bytes=ALIGN)
+            smaller, larger = extremes[:, 0], extremes[:, 1]
+            bank = psum.tile([P, PACK, W], F32, name="a_bank", tag=f"a{chunk}")
+            products(bank, query_q, keys_q, slots(chunk))
+            nc.vector.tensor_tensor(smaller, bank[:], b_chunks[chunk][:], ALU.min)
+            nc.vector.tensor_tensor(larger, bank[:], b_chunks[chunk][:], ALU.max)
+            scores = sbuf.tile([P, PACK, W], F32, name=f"scores{chunk}", align_bytes=ALIGN)
             for t in range(PACK):
                 nc.vector.scalar_tensor_tensor(
                     scores[:, t, :], smaller[:, t, :], lam_cols[:, t : t + 1], larger[:, t, :], ALU.mult, ALU.add
                 )
-            w = keep.tile([P, W, PACK], F32, name="w", tag=["r1","w1","w2","w3"][chunk], align_bytes=64)
+            w_tag = f"w{chunk}" if chunk > 0 else "chain"
+            w = sbuf.tile([P, W, PACK], F32, name="w", tag=w_tag, align_bytes=ALIGN)
             nc.scalar.activation(w[:], scores[:].rearrange("p t i -> p i t"), ACT.Sigmoid)
             weights.append(w)
 
-        dl_banks = []
-
         def weigh(chunk):
-            wq = keep.tile([P, W, PACK], BF16, name="wq", tag=["q0","q1","q2","q3"][chunk], align_bytes=64)
+            wq = sbuf.tile([P, W, PACK], BF16, name=f"wq{chunk}", align_bytes=ALIGN)
             nc.vector.tensor_tensor(
                 wq[:], weights[chunk][:], qs_cols[:].unsqueeze(1).to_broadcast([P, W, PACK]), ALU.mult
             )
             wq_q = quantise(f"wq{chunk}", wq[:].rearrange("p i t -> p (i t)"), W)
-            bank = psum.tile([P, 4, W], F32, name="dl_bank", tag=f"low{chunk}")
+            bank = psum.tile([P, ROW_TILES, W], F32, name="dl_bank", tag=f"dl{chunk}")
             products(bank, msgs_q, wq_q, slice(0, W))
             dl_banks.append(bank)
 
-        dl = keep.tile([P, 4, I], F32, name="dl")
+        def empty(chunk, copy, first, last, tag):
+            dl = sbuf.tile([P, last - first, W], F32, name="dl", tag=tag, align_bytes=ALIGN)
+            copy(out=dl[:], in_=dl_banks[chunk][:, first:last, :])
+            for k in range(first, last):
+                sums[k, chunk] = dl[:, k - first, :]
 
-        def empty(chunk, copy, first=0, last=4):
-            copy(out=dl[:, first:last, chunk * W : (chunk + 1) * W], in_=dl_banks[chunk][:, first:last, :])
+        late_sums = sbuf.tile([P, I - W], F32, name="late_sums")
 
-        def scatter(k, first, last, on_vector):
-            window = windows[k][:].indirect(entries(place_list, first, last))
-            source = dl[:, k, first:last]
-            if on_vector:
-                nc.vector.tensor_copy(window, source)
-            else:
-                nc.scalar.activation(window, source, ACT.Copy)
+        def empty_later_chunk(chunk, copy, tag):
+            empty(chunk, copy, 0, LAST, tag)
+            copy(out=late_sums[:, slots(chunk - 1)], in_=dl_banks[chunk][:, LAST, :])
 
-        def finish(k, first, last, engine):
-            engine.tensor_tensor(olds[k][:, first:last], olds[k][:, first:last], windows[k][:, first:last], ALU.add)
-            nc.sync.dma_start(out[k * P : (k + 1) * P, first:last], olds[k][:, first:last])
+        def scatter(k, first, last, source):
+            window = delivered[k][:].indirect(entries(place_list, first, last))
+            nc.scalar.activation(window, source, ACT.Copy)
 
-        def faded(k):
-            for h in range(2):
-                cols = slice(h * 512, (h + 1) * 512)
-                nc.vector.tensor_tensor(
-                    olds[k][:, cols], olds[k][:, cols], fade_banks[h][:].rearrange("p c m -> p (c m)"), ALU.mult
-                )
+        second_scores(0)
+        msgs_grouped = sbuf.tile([P, E, PACK], BF16, name="msgs_grouped", align_bytes=ALIGN)
+        for cols, raw in zip(msgs_halves, msgs_raw):
+            interleave(nc.scalar.copy, msgs_grouped[:, cols, :], raw[:])
 
-        pick_words(0 * W, 1 * W)
+        pick_words(0, W)
         score(0)
-        pick_words(1 * W, 4 * W)
+        pick_words(W, I)
         msgs_q = quantise("msgs", msgs_grouped[:].rearrange("p e j -> p (e j)"), E)
         weigh(0)
-        empty(0, nc.scalar.copy, 0, 2)
+        empty(0, nc.scalar.copy, 0, ROW_TILES // 2, "sums0")
+        second_scores(1)
         score(1)
-        empty(0, nc.vector.tensor_copy, 2, 4)
+        empty(0, nc.scalar.copy, ROW_TILES // 2, ROW_TILES, "scores1")
         weigh(1)
+        second_scores(2)
         score(2)
-        empty(1, nc.scalar.copy, 0, 4)
+        empty_later_chunk(1, nc.scalar.copy, "scores2")
         weigh(2)
+        second_scores(3)
         score(3)
-        empty(2, nc.vector.tensor_copy, 0, 4)
+        empty_later_chunk(2, nc.vector.tensor_copy, "chain")
         weigh(3)
-        empty(3, nc.scalar.copy, 0, 4)
-        turned = psum.tile([P, P], F32, name="turned", tag="high0")
+        empty_later_chunk(3, nc.scalar.copy, "sums3")
+
+        turned = psum.tile([P, P], F32, name="turned", tag="a0")
         nc.tensor.transpose(turned[:], fade_rows[:], identity[:])
-        fade_cols = keep.tile([P, M // P], F32, name="fade_cols")
+        fade_cols = sbuf.tile([P, M // P], F32, name="fade_cols")
         nc.vector.tensor_copy(fade_cols[:], turned[:, 0 : M // P])
-        fade_banks = [psum.tile([P, 4, P], F32, name=f"fade_bank{h}", tag=f"high{h + 2}") for h in range(2)]
+        per_bank = HALF // P
+        fade_banks = [psum.tile([P, per_bank, P], F32, name="fade_bank", tag=tag) for tag in ("a2", "a3")]
         for c in range(M // P):
             nc.tensor.transpose(
-                fade_banks[c // 4][:, c % 4, :], fade_cols[:, c : c + 1].to_broadcast([P, P]), identity[:]
+                fade_banks[c // per_bank][:, c % per_bank, :],
+                fade_cols[:, c : c + 1].to_broadcast([P, P]),
+                identity[:],
             )
-        scatter(0, 0 * W, 1 * W, False)
-        scatter(1, 0 * W, 1 * W, False)
-        scatter(2, 0 * W, 1 * W, False)
-        scatter(3, 0 * W, 1 * W, False)
-        scatter(0, 1 * W, 2 * W, False)
-        scatter(1, 1 * W, 2 * W, False)
-        scatter(2, 1 * W, 2 * W, False)
-        scatter(0, 2 * W, 3 * W, False)
-        scatter(1, 2 * W, 3 * W, False)
-        scatter(2, 2 * W, 3 * W, False)
-        faded(0)
-        faded(1)
-        faded(2)
-        faded(3)
-        scatter(0, 3 * W, 4 * W, False)
-        finish(0, 0, M // 2, nc.vector)
-        finish(0, M // 2, M, nc.vector)
-        scatter(1, 3 * W, 4 * W, False)
-        finish(1, 0, M // 2, nc.vector)
-        finish(1, M // 2, M, nc.vector)
-        scatter(2, 3 * W, 4 * W, False)
-        finish(2, 0, M // 2, nc.vector)
-        finish(2, M // 2, M, nc.vector)
-        scatter(3, 1 * W, 4 * W, False)
-        finish(3, 0, M // 2, nc.vector)
-        finish(3, M // 2, M, nc.vector)
+
+        for chunk in range(CHUNKS - 1):
+            for k in range(ROW_TILES if chunk == 0 else LAST):
+                scatter(k, chunk * W, (chunk + 1) * W, sums[k, chunk])
+        halves = [slice(0, HALF), slice(HALF, M)]
+        for k in range(ROW_TILES):
+            for cols, bank in zip(halves, fade_banks):
+                faded = results[k][:, cols]
+                nc.vector.tensor_tensor(faded, faded, bank[:].rearrange("p c m -> p (c m)"), ALU.mult)
+        for k in range(ROW_TILES):
+            if k < LAST:
+                scatter(k, I - W, I, sums[k, CHUNKS - 1])
+            else:
+                scatter(k, W, I, late_sums[:])
+            for cols in halves:
+                total = results[k][:, cols]
+                nc.vector.tensor_tensor(total, total, delivered[k][:, cols], ALU.add)
+                nc.sync.dma_start(out[k * P : (k + 1) * P, cols], total)

from contextlib import ExitStack

import concourse.mybir as mybir
from concourse.masks import make_identity

D, T, I, Q, E, U, M = 512, 2048, 512, 512, 512, 1024, 1024
FLOPS = 2 * (D * Q * I + D * Q * I + Q * E * I)

F32 = mybir.dt.float32
BF16 = mybir.dt.bfloat16
I32 = mybir.dt.int32
U32 = mybir.dt.uint32
U16 = mybir.dt.uint16
U8 = mybir.dt.uint8
FP8X4 = mybir.dt.float8_e4m3fn_x4
ALU = mybir.AluOpType
ACT = mybir.ActivationFunctionType

P = 128
PACK = 4
LIST_ROWS = 16
QUADRANT = 32
ALIGN = 64
CHUNKS = 4
W = I // CHUNKS
ROW_TILES = E // P
LAST = ROW_TILES - 1
HALF = M // 2

SCALAR_NOTE_ENTRIES = (I, 0, I, I // 4)
SCALAR_NOTE_SLOTS = 160
SCALAR_QUERY_ROWS = P // 2


def tile_attend_twopools_delivered_lean_kernel(
    tc, query, keys_words, keys_scales, query2, notes, lam, qs, msgs, old, fade, offs, offs2, offs3, out
):
    nc = tc.nc
    with ExitStack() as ctx:
        sbuf = ctx.enter_context(tc.tile_pool(name="sbuf", bufs=1))
        psum = ctx.enter_context(tc.psum_pool(name="psum", bufs=1))

        def quantise(name, grouped, width):
            codes = sbuf.tile([P, width], U32, name=name + "_codes", align_bytes=ALIGN)
            scales = sbuf.tile([P, width], U8, name=name + "_scales", align_bytes=ALIGN)
            nc.vector.quantize_mx(out=codes[:].bitcast(FP8X4), scales=scales[:], in_=grouped)
            return codes, scales

        def products(bank, stationary, moving, moving_cols):
            for r in range(bank.shape[1]):
                cols = slice(r * P, (r + 1) * P)
                nc.tensor.matmul_mx(
                    out=bank[:, r, :],
                    lhsT=stationary[0][:, cols].bitcast(FP8X4),
                    lhsT_scale=stationary[1][:, cols],
                    rhs=moving[0][:, moving_cols].bitcast(FP8X4),
                    rhs_scale=moving[1][:, moving_cols],
                    start=True,
                    stop=True,
                )

        def entries(list_tile, first, last):
            return list_tile[:, first // LIST_ROWS : last // LIST_ROWS]

        def slots(chunk):
            return slice(chunk * W, (chunk + 1) * W)

        key_bytes = sbuf.tile([P, T], U8, name="key_bytes", align_bytes=ALIGN)
        nc.gpsimd.memset(key_bytes[:].bitcast(I32), 0)

        warm_in = sbuf.tile([P, 1], F32, name="warm_in")
        warm_out = sbuf.tile([P, 1], F32, name="warm_out")
        nc.gpsimd.memset(warm_in[:], 0.0)
        nc.scalar.activation(warm_out[:], warm_in[:], ACT.Sigmoid)

        delivered = [sbuf.tile([P, M], F32, name=f"delivered{k}") for k in range(ROW_TILES)]
        for k in range(ROW_TILES):
            (nc.vector if k < ROW_TILES // 2 else nc.gpsimd).memset(delivered[k][:], 0.0)
        fade_rows = sbuf.tile([P, P], F32, name="fade_rows")
        nc.vector.memset(fade_rows[:], 0.0)

        query2_raw = sbuf.tile([P, PACK, Q], F32, name="query2_raw")
        nc.sync.dma_start(query2_raw[:], query2.rearrange("(p j) q -> p j q", j=PACK))
        note_list = sbuf.tile([P, I // LIST_ROWS], U16, name="note_list")
        nc.sync.dma_start(note_list[:], offs2)
        note_rows = notes.rearrange("(p j) u -> p j u", j=PACK)
        note_planes = [sbuf.tile([P, U], F32, name=f"note_plane{j}") for j in range(PACK)]
        key_list = sbuf.tile([P, I // LIST_ROWS], U16, name="key_list")
        nc.sync.dma_start(note_planes[0][:], note_rows[:, 0, :])
        nc.sync.dma_start(key_list[:], offs)
        for j in range(PACK):
            nc.sync.dma_start(
                key_bytes[j:P:QUADRANT, :].bitcast(I32), keys_scales[0, j : D // 32 : PACK, :].bitcast(I32)
            )
            if j > 0:
                nc.sync.dma_start(note_planes[j][:], note_rows[:, j, :])
        query_raw = sbuf.tile([P, PACK, Q], F32, name="query_raw")
        nc.sync.dma_start(query_raw[:], query.rearrange("(p j) q -> p j q", j=PACK))
        key_words = sbuf.tile([P, T], U32, name="key_words")
        nc.sync.dma_start(key_words[:].bitcast(I32), keys_words[0].rearrange("p n t -> p (n t)").bitcast(I32))
        lam_cols = sbuf.tile([P, PACK], F32, name="lam_cols")
        nc.sync.dma_start(lam_cols[:], lam.rearrange("(p t) o -> p (t o)", t=PACK))
        msgs_rows = msgs.rearrange("(p j) e -> p j e", j=PACK)
        msgs_halves = [slice(0, E // 2), slice(E // 2, E)]
        msgs_raw = []
        for cols, tag in zip(msgs_halves, ("msgs_first", "chain")):
            raw = sbuf.tile([P, PACK, E // 2], F32, name="msgs_raw", tag=tag, align_bytes=ALIGN)
            nc.sync.dma_start(raw[:], msgs_rows[:, :, cols])
            msgs_raw.append(raw)
        qs_cols = sbuf.tile([P, PACK], F32, name="qs_cols")
        nc.sync.dma_start(qs_cols[:], qs.rearrange("(p t) o -> p (t o)", t=PACK))
        place_list = sbuf.tile([P, I // LIST_ROWS], U16, name="place_list")
        nc.sync.dma_start(place_list[:], offs3)
        nc.sync.dma_start(fade_rows[0 : M // P, :], fade[0].rearrange("(c p) -> c p", p=P))
        identity = sbuf.tile([P, P], F32, name="identity")
        make_identity(nc, identity[:])
        results = [sbuf.tile([P, M], F32, name=f"result{k}") for k in range(ROW_TILES)]
        for k in range(ROW_TILES):
            nc.sync.dma_start(results[k][:], old[k * P : (k + 1) * P, :])

        def deal(copy, grouped, raw, first, last):
            copy(
                out=grouped[:].rearrange("p t m j -> p m t j")[:, first:last],
                in_=raw[:].rearrange("p j (m t) -> p m t j", t=PACK)[:, first:last],
            )

        def interleave(copy, grouped, planes):
            copy(
                out=grouped.rearrange("p (c i) j -> p c j i", i=PACK),
                in_=planes.rearrange("p j (c i) -> p c j i", i=PACK),
            )

        query2_grouped = sbuf.tile([P, PACK, P, PACK], BF16, name="query2_grouped", align_bytes=ALIGN)
        deal(nc.vector.tensor_copy, query2_grouped, query2_raw, 0, P)
        query2_q = quantise("query2", query2_grouped[:].rearrange("p t m j -> p (t m j)"), Q)

        picked_bytes = sbuf.tile([P, I], U8, name="picked_bytes", align_bytes=ALIGN)
        nc.vector.tensor_copy(picked_bytes[:], key_bytes[:].indirect(key_list[:]))

        picked_notes = sbuf.tile([P, PACK, I], BF16, name="picked_notes")
        for j, split in enumerate(SCALAR_NOTE_ENTRIES):
            if split > 0:
                window = note_planes[j][:].indirect(entries(note_list, 0, split))
                nc.scalar.activation(picked_notes[:, j, :split], window, ACT.Copy)
            if split < I:
                window = note_planes[j][:].indirect(entries(note_list, split, I))
                nc.vector.tensor_copy(picked_notes[:, j, split:], window)
        notes_grouped = sbuf.tile([P, I, PACK], BF16, name="notes_grouped", align_bytes=ALIGN)
        for copy, cols in (
            (nc.scalar.copy, slice(0, SCALAR_NOTE_SLOTS)),
            (nc.vector.tensor_copy, slice(SCALAR_NOTE_SLOTS, I)),
        ):
            interleave(copy, notes_grouped[:, cols, :], picked_notes[:, :, cols])
        notes_q = quantise("notes", notes_grouped[:].rearrange("p i j -> p (i j)"), I)

        query_grouped = sbuf.tile([P, PACK, P, PACK], BF16, name="query_grouped", align_bytes=ALIGN)
        deal(nc.scalar.copy, query_grouped, query_raw, 0, SCALAR_QUERY_ROWS)
        deal(nc.vector.tensor_copy, query_grouped, query_raw, SCALAR_QUERY_ROWS, P)
        query_q = quantise("query", query_grouped[:].rearrange("p t m j -> p (t m j)"), Q)

        picked_words = sbuf.tile([P, I], U32, name="picked_words", align_bytes=ALIGN)
        keys_q = (picked_words, picked_bytes)

        def pick_words(first, last):
            nc.vector.tensor_copy(picked_words[:, first:last], key_words[:].indirect(entries(key_list, first, last)))

        b_tags = ("b0", "b1", "scores0", "msgs_grouped")
        b_bank_tags = ("dl0", "dl1", "a0", "dl3")
        b_chunks, weights, dl_banks, sums = [], [], [], {}

        def second_scores(chunk):
            bank = psum.tile([P, PACK, W], F32, name="b_bank", tag=b_bank_tags[chunk])
            products(bank, query2_q, notes_q, slots(chunk))
            b_chunk = sbuf.tile([P, PACK, W], F32, name="b_chunk", tag=b_tags[chunk], align_bytes=ALIGN)
            nc.scalar.copy(out=b_chunk[:], in_=bank[:])
            b_chunks.append(b_chunk)

        def score(chunk):
            extremes_tag = "chain" if chunk > 0 else "extremes0"
            extremes = sbuf.tile([P, 2, PACK, W], F32, name="extremes", tag=extremes_tag, align_bytes=ALIGN)
            smaller, larger = extremes[:, 0], extremes[:, 1]
            bank = psum.tile([P, PACK, W], F32, name="a_bank", tag=f"a{chunk}")
            products(bank, query_q, keys_q, slots(chunk))
            nc.vector.tensor_tensor(smaller, bank[:], b_chunks[chunk][:], ALU.min)
            nc.vector.tensor_tensor(larger, bank[:], b_chunks[chunk][:], ALU.max)
            scores = sbuf.tile([P, PACK, W], F32, name=f"scores{chunk}", align_bytes=ALIGN)
            for t in range(PACK):
                nc.vector.scalar_tensor_tensor(
                    scores[:, t, :], smaller[:, t, :], lam_cols[:, t : t + 1], larger[:, t, :], ALU.mult, ALU.add
                )
            w_tag = f"w{chunk}" if chunk > 0 else "chain"
            w = sbuf.tile([P, W, PACK], F32, name="w", tag=w_tag, align_bytes=ALIGN)
            nc.scalar.activation(w[:], scores[:].rearrange("p t i -> p i t"), ACT.Sigmoid)
            weights.append(w)

        def weigh(chunk):
            wq = sbuf.tile([P, W, PACK], BF16, name=f"wq{chunk}", align_bytes=ALIGN)
            nc.vector.tensor_tensor(
                wq[:], weights[chunk][:], qs_cols[:].unsqueeze(1).to_broadcast([P, W, PACK]), ALU.mult
            )
            wq_q = quantise(f"wq{chunk}", wq[:].rearrange("p i t -> p (i t)"), W)
            bank = psum.tile([P, ROW_TILES, W], F32, name="dl_bank", tag=f"dl{chunk}")
            products(bank, msgs_q, wq_q, slice(0, W))
            dl_banks.append(bank)

        def empty(chunk, copy, first, last, tag):
            dl = sbuf.tile([P, last - first, W], F32, name="dl", tag=tag, align_bytes=ALIGN)
            copy(out=dl[:], in_=dl_banks[chunk][:, first:last, :])
            for k in range(first, last):
                sums[k, chunk] = dl[:, k - first, :]

        late_sums = sbuf.tile([P, I - W], F32, name="late_sums")

        def empty_later_chunk(chunk, copy, tag):
            empty(chunk, copy, 0, LAST, tag)
            copy(out=late_sums[:, slots(chunk - 1)], in_=dl_banks[chunk][:, LAST, :])

        def scatter(k, first, last, source):
            window = delivered[k][:].indirect(entries(place_list, first, last))
            nc.scalar.activation(window, source, ACT.Copy)

        second_scores(0)
        msgs_grouped = sbuf.tile([P, E, PACK], BF16, name="msgs_grouped", align_bytes=ALIGN)
        for cols, raw in zip(msgs_halves, msgs_raw):
            interleave(nc.scalar.copy, msgs_grouped[:, cols, :], raw[:])

        pick_words(0, W)
        score(0)
        pick_words(W, I)
        msgs_q = quantise("msgs", msgs_grouped[:].rearrange("p e j -> p (e j)"), E)
        weigh(0)
        empty(0, nc.scalar.copy, 0, ROW_TILES // 2, "sums0")
        second_scores(1)
        score(1)
        empty(0, nc.scalar.copy, ROW_TILES // 2, ROW_TILES, "scores1")
        weigh(1)
        second_scores(2)
        score(2)
        empty_later_chunk(1, nc.scalar.copy, "scores2")
        weigh(2)
        second_scores(3)
        score(3)
        empty_later_chunk(2, nc.vector.tensor_copy, "chain")
        weigh(3)
        empty_later_chunk(3, nc.scalar.copy, "sums3")

        turned = psum.tile([P, P], F32, name="turned", tag="a0")
        nc.tensor.transpose(turned[:], fade_rows[:], identity[:])
        fade_cols = sbuf.tile([P, M // P], F32, name="fade_cols")
        nc.vector.tensor_copy(fade_cols[:], turned[:, 0 : M // P])
        per_bank = HALF // P
        fade_banks = [psum.tile([P, per_bank, P], F32, name="fade_bank", tag=tag) for tag in ("a2", "a3")]
        for c in range(M // P):
            nc.tensor.transpose(
                fade_banks[c // per_bank][:, c % per_bank, :],
                fade_cols[:, c : c + 1].to_broadcast([P, P]),
                identity[:],
            )

        for chunk in range(CHUNKS - 1):
            for k in range(ROW_TILES if chunk == 0 else LAST):
                scatter(k, chunk * W, (chunk + 1) * W, sums[k, chunk])
        halves = [slice(0, HALF), slice(HALF, M)]
        for k in range(ROW_TILES):
            for cols, bank in zip(halves, fade_banks):
                faded = results[k][:, cols]
                nc.vector.tensor_tensor(faded, faded, bank[:].rearrange("p c m -> p (c m)"), ALU.mult)
        for k in range(ROW_TILES):
            if k < LAST:
                scatter(k, I - W, I, sums[k, CHUNKS - 1])
            else:
                scatter(k, W, I, late_sums[:])
            for cols in halves:
                total = results[k][:, cols]
                nc.vector.tensor_tensor(total, total, delivered[k][:, cols], ALU.add)
                nc.sync.dma_start(out[k * P : (k + 1) * P, cols], total)
